import numpy as np
import ml_dtypes


def mxq(x, axis, fmt="e4m3"):
    dtype, down = {"e4m3": (ml_dtypes.float8_e4m3fn, 7), "e5m2": (ml_dtypes.float8_e5m2, 14)}[fmt]
    v = np.moveaxis(np.asarray(x, np.float32).astype(ml_dtypes.bfloat16).astype(np.float64), axis, -1)
    blocks = v.reshape(v.shape[:-1] + (-1, 32))
    amax = np.abs(blocks).max(-1, keepdims=True)
    byte = np.maximum(np.where(amax > 0, np.frexp(amax)[1] - 1 + 127, 0) - down, 1)
    scale = np.exp2(byte - 127.0)
    codes = (blocks / scale).astype(np.float32).astype(dtype).astype(np.float64)
    return np.moveaxis((codes * scale).reshape(v.shape), -1, axis)


WIDE = False


def mx_kscale(k):
    if not WIDE:
        return np.ones(k)
    levels = np.array([10, -10, 5, -5, 0])
    if k % 512:
        return np.exp2(np.random.permutation(np.resize(levels, k // 32))).repeat(32)
    a = np.empty((k // 512, 16))
    for p in range(k // 512):
        a[p, :8] = np.random.permutation(np.resize(levels, 8))
        for g in range(8):
            far = levels[np.abs(levels - a[p, g]) >= 10]
            a[p, g + 8] = far[np.random.randint(len(far))]
    return np.exp2(a.ravel()).repeat(32)


def f64(x):
    return np.asarray(x).astype(np.float64)


def striped(idx):
    return np.tile(np.asarray(idx).reshape(-1, 16).T, (8, 1)).astype(np.uint16)


def unstriped(offs):
    return offs[:16].T.reshape(-1).astype(np.int64)


E2M1 = np.array([0.0, 0.5, 1.0, 1.5, 2.0, 3.0, 4.0, 6.0, -0.0, -0.5, -1.0, -1.5, -2.0, -3.0, -4.0, -6.0])


def pack_weight(w, fmt):
    k, n = w.shape
    w = f64(np.asarray(w, np.float32).astype(ml_dtypes.bfloat16)).reshape(k // 32, 32, n)
    amax = np.abs(w).max(1)
    if fmt == "e4m3":
        byte = np.frexp(amax)[1] - 1 + 127 - 7
    else:
        mant, ex = np.frexp(amax / 6.0)
        byte = np.where(mant > 0.5, ex, ex - 1) + 127
    byte = np.clip(np.where(amax > 0, byte, 1), 1, 254)
    scaled = (w * np.exp2(127.0 - byte)[:, None, :]).reshape(k, n).astype(np.float32)
    by_word = np.ascontiguousarray(scaled.reshape(k // 512, 128, 4, n).transpose(0, 1, 3, 2))
    if fmt == "e4m3":
        words = by_word.astype(ml_dtypes.float8_e4m3fn).view(np.uint8)
    else:
        c = by_word.astype(ml_dtypes.float4_e2m1fn).view(np.uint8) & 0xF
        words = (c[..., 0::2] | (c[..., 1::2] << 4)).reshape(k // 512, 128, 2 * n)
    return np.ascontiguousarray(words), np.ascontiguousarray(byte.astype(np.uint8).reshape(k // 512, 16, n))


def unpack_weight(words, scales, fmt):
    g, _, n = scales.shape
    words = np.ascontiguousarray(words).reshape(g, 128, n, -1)
    if fmt == "e4m3":
        vals = words.view(ml_dtypes.float8_e4m3fn).astype(np.float64)
    else:
        nib = np.empty((g, 128, n, 4), np.uint8)
        nib[..., 0::2] = words & 0xF
        nib[..., 1::2] = words >> 4
        vals = E2M1[nib]
    vals = vals * np.repeat(np.exp2(scales.astype(np.float64) - 127.0), 8, axis=1)[..., None]
    return vals.transpose(0, 1, 3, 2).reshape(g * 512, n)


def bf(x):
    return np.asarray(x, np.float32).astype(ml_dtypes.bfloat16)


def planes(Y):
    r, m = Y.shape
    b = f64(bf(Y)).reshape(r // 32, 32, m)
    amax = np.abs(b).max(1)
    byte = np.clip(np.where(amax > 0, np.frexp(amax)[1] - 1 + 127 - 7, 1), 1, 254)
    codes = (b * np.exp2(127.0 - byte)[:, None, :]).reshape(r, m).astype(np.float32).astype(ml_dtypes.float8_e4m3fn).view(np.uint8)
    words = codes.reshape(r // 512, 128, 4, m).transpose(0, 1, 3, 2)
    return np.ascontiguousarray(words), np.ascontiguousarray(byte.astype(np.uint8).reshape(r // 512, 16, m))


K, L, T, J, N = 512, 512, 1024, 512, 512


def setup_inputs():
    n = np.random.standard_normal
    idx = np.random.permutation(T)[:J]
    idx2 = np.random.permutation(T)[:J]
    fk = mx_kscale(K)
    fl = mx_kscale(L)
    wpp = pack_weight(n((K, N)) * 1 / np.sqrt(K) * fk[:, None], "e4m3")
    xtp = pack_weight(n((L, J)) / fl[:, None], "e2m1")
    wxp = pack_weight(n((L, N)) * 1 / np.sqrt(L) * fl[:, None], "e4m3")
    return {
        "page": (n((K, T)) / fk[:, None]).astype(np.float32),
        "wp_words": wpp[0],
        "wp_scales": wpp[1],
        "xt_words": xtp[0],
        "xt_scales": xtp[1],
        "wx_words": wxp[0],
        "wx_scales": wxp[1],
        "old": (1.0 * n((N, T))).astype(np.float32),
        "offs": striped(idx),
        "offs2": striped(idx2),
    }


def reference(page, wp_words, wp_scales, xt_words, xt_scales, wx_words, wx_scales, old, offs, offs2):
    idx = unstriped(offs)
    idx2 = unstriped(offs2)
    wpu = unpack_weight(wp_words, wp_scales, "e4m3")
    xtu = unpack_weight(xt_words, xt_scales, "e2m1")
    wxu = unpack_weight(wx_words, wx_scales, "e4m3")
    pageidxq = mxq(f64(page)[:, idx], 0, "e4m3")
    z = wpu.T @ pageidxq + wxu.T @ xtu
    h1 = np.tanh(z)
    p = np.zeros((N, T))
    p[:, idx2] = h1
    y = 0.3 * f64(old) + p
    words, scales = planes(y)
    return y, words, scales

@@ -1,0 +1,167 @@
+from contextlib import ExitStack
+
+import concourse.mybir as mybir
+
+K, L, T, J, N = 512, 512, 1024, 512, 512
+FLOPS = 2 * N * J * (K + L)
+
+F32 = mybir.dt.float32
+BF16 = mybir.dt.bfloat16
+I32 = mybir.dt.int32
+U32 = mybir.dt.uint32
+U16 = mybir.dt.uint16
+U8 = mybir.dt.uint8
+FP8X4 = mybir.dt.float8_e4m3fn_x4
+FP4X4 = mybir.dt.float4_e2m1fn_x4
+MULT = mybir.AluOpType.mult
+ADD = mybir.AluOpType.add
+TANH = mybir.ActivationFunctionType.Tanh
+
+P = 128
+PACK = 4
+PER_COL = 16
+CH = 256
+NCH = J // CH
+QW = 256
+NQ = T // QW
+OLD_SCALE = 0.3
+
+
+def tile_list_read_write_page_pl_kernel(tc, page, wp_words, wp_scales, xt_words, xt_scales, wx_words, wx_scales,
+                                           old, offs, offs2, out_0, out_1, out_2):
+    nc = tc.nc
+    with ExitStack() as ctx:
+        lists = ctx.enter_context(tc.tile_pool(name="lists", bufs=1))
+        sb = ctx.enter_context(tc.tile_pool(name="sb", bufs=1))
+        psum = ctx.enter_context(tc.psum_pool(name="psum", bufs=1))
+
+        read_list = lists.tile([P, J // PER_COL], U16, name="read_list")
+        write_list = lists.tile([P, J // PER_COL], U16, name="write_list")
+
+        sc_raw = sb.tile([P, N + J], U8, name="sc_raw", align_bytes=64)
+        nc.gpsimd.memset(sc_raw[:].bitcast(U32), 0)
+        w_sc_raw = sc_raw[:, 0:N]
+
+        page_rows = page.rearrange("(p r) t -> p r t", r=PACK)
+        old_rows = old.rearrange("(p r) t -> p r t", r=PACK)
+        out_rows = out_0.rearrange("(p r) t -> p r t", r=PACK)
+
+        def load_scales(eng, src, q, row0, col0):
+            eng.dma_start(sc_raw[32 * q + row0 : 32 * q + row0 + 4, col0 : col0 + N].bitcast(I32),
+                          src[0, 4 * q : 4 * q + 4, :].bitcast(I32))
+
+        pg = [sb.tile([P, T], F32, name="pg%d" % r) for r in range(PACK)]
+        wp_raw = sb.tile([P, N], I32, name="wp_raw", align_bytes=64)
+        wx_raw = sb.tile([P, N], I32, name="wx_raw", align_bytes=64)
+        xt_codes = sb.tile([P, 2 * J], U8, name="xt_codes", align_bytes=64)
+        nc.sync.dma_start(read_list[:], offs)
+        nc.sync.dma_start(pg[0][:], page_rows[:, 0, :])
+        for q in range(3):
+            load_scales(nc.sync, wp_scales, q, 4, 0)
+        for r in range(1, PACK):
+            nc.sync.dma_start(pg[r][:], page_rows[:, r, :])
+        for q in range(4):
+            load_scales(nc.sync, wx_scales, q, 0, 0)
+        load_scales(nc.gpsimd, wp_scales, 3, 4, 0)
+        for q in range(4):
+            load_scales(nc.gpsimd, xt_scales, q, 0, N)
+        nc.sync.dma_start(wp_raw[:], wp_words[0].rearrange("p n t -> p (n t)").bitcast(I32))
+        nc.sync.dma_start(wx_raw[:], wx_words[0].rearrange("p n t -> p (n t)").bitcast(I32))
+        nc.sync.dma_start(xt_codes[:].bitcast(I32), xt_words[0].bitcast(I32))
+        nc.sync.dma_start(write_list[:], offs2)
+        od = [sb.tile([P, T], F32, name="od%d" % r) for r in range(PACK)]
+        for r in range(PACK):
+            nc.sync.dma_start(od[r][:], old_rows[:, r, :])
+
+        warm = sb.tile([P, 8], F32, name="warm")
+        warm_out = sb.tile([P, 8], F32, name="warm_out")
+        nc.vector.memset(warm[:], 0.0)
+        nc.scalar.activation(warm_out[:], warm[:], TANH)
+
+        placed = [sb.tile([P, T], F32, name="placed%d" % r) for r in range(PACK)]
+        for r in range(PACK):
+            (nc.vector if r < 2 else nc.gpsimd).memset(placed[r][:], 0.0)
+
+        def entries(lst, c):
+            return lst[:, c * CH // PER_COL : (c + 1) * CH // PER_COL]
+
+        g01 = sb.tile([P, 2, J], F32, name="g01")
+        g23 = [sb.tile([P, 2, CH], F32, name="g23_%d" % c) for c in range(NCH)]
+        xb = [sb.tile([P, CH, PACK], BF16, name="xb%d" % c, align_bytes=64) for c in range(NCH)]
+        for r in range(2):
+            nc.vector.tensor_copy(g01[:, r, :], pg[r][:].indirect(read_list[:]))
+        for c in range(NCH):
+            nc.scalar.copy(xb[c][:, :, 0:2], g01[:, :, c * CH : (c + 1) * CH].rearrange("p r j -> p j r"))
+        for r in range(2, PACK):
+            for c in range(NCH):
+                nc.vector.tensor_copy(g23[c][:, r - 2, :], pg[r][:].indirect(entries(read_list, c)))
+        for c in range(NCH):
+            nc.scalar.copy(xb[c][:, :, 2:4], g23[c][:].rearrange("p r j -> p j r"))
+
+        w_sc = sb.tile([P, PACK, P], U8, name="w_sc", align_bytes=64)
+        wp_codes = sb.tile([P, PACK, P], I32, name="wp_codes", align_bytes=64)
+        wx_codes = sb.tile([P, PACK, P], I32, name="wx_codes", align_bytes=64)
+        nc.vector.tensor_copy(w_sc[:], w_sc_raw.rearrange("p (m r) -> p r m", r=PACK))
+        nc.vector.tensor_copy(wp_codes[:], wp_raw[:].rearrange("p (m r) -> p r m", r=PACK))
+        nc.vector.tensor_copy(wx_codes[:], wx_raw[:].rearrange("p (m r) -> p r m", r=PACK))
+
+        xq = [sb.tile([P, CH], U32, name="xq%d" % c, align_bytes=64) for c in range(NCH)]
+        xs = [sb.tile([P, CH], U8, name="xs%d" % c, align_bytes=64) for c in range(NCH)]
+        for c in range(NCH):
+            nc.vector.quantize_mx(out=xq[c][:].bitcast(FP8X4), scales=xs[c][:], in_=xb[c][:].rearrange("p j r -> p (j r)"))
+
+        h = [sb.tile([P, J], F32, name="h%d" % r) for r in range(PACK)]
+
+        def product(r, c):
+            z = psum.tile([P, CH], F32, name="z%d_%d" % (r, c))
+            nc.tensor.matmul_mx(out=z[:], lhsT=wp_codes[:, r, :].bitcast(FP8X4), lhsT_scale=w_sc[4:P, r, :],
+                                rhs=xq[c][:].bitcast(FP8X4), rhs_scale=xs[c][:], start=True, stop=False)
+            for u in range(CH // P):
+                j0 = c * CH + u * P
+                nc.tensor.matmul_mx(out=z[:, u * P : (u + 1) * P], lhsT=wx_codes[:, r, :].bitcast(FP8X4),
+                                    lhsT_scale=w_sc[:, r, :], rhs=xt_codes[:, 2 * j0 : 2 * (j0 + P)].bitcast(FP4X4),
+                                    rhs_scale=sc_raw[:, N + j0 : N + j0 + P], start=False, stop=(u == CH // P - 1))
+            nc.scalar.activation(h[r][:, c * CH : (c + 1) * CH], z[:], TANH)
+
+        for r, c in ((0, 0), (1, 0), (0, 1), (1, 1)):
+            product(r, c)
+            nc.vector.tensor_copy(placed[r][:].indirect(entries(write_list, c)), h[r][:, c * CH : (c + 1) * CH])
+        for r in (2, 3):
+            for c in range(NCH):
+                product(r, c)
+            nc.vector.tensor_copy(placed[r][:].indirect(write_list[:]), h[r][:])
+
+        scaled = [sb.tile([P, T], F32, name="scaled%d" % r) for r in range(3)]
+        y01 = sb.tile([P, 2, T], F32, name="y01")
+        y23 = [sb.tile([P, 2, QW], F32, name="y23_%d" % q) for q in range(NQ)]
+        yb = [sb.tile([P, QW, PACK], BF16, name="yb%d" % q, align_bytes=64) for q in range(NQ)]
+        yq = [sb.tile([P, QW], U32, name="yq%d" % q, align_bytes=64) for q in range(NQ)]
+        ys = sb.tile([P, T], U8, name="ys", align_bytes=64)
+        for r in range(3):
+            nc.gpsimd.tensor_scalar(scaled[r][:], od[r][:], OLD_SCALE, 0.0, MULT, ADD)
+        for r in range(2):
+            nc.gpsimd.tensor_tensor(y01[:, r, :], placed[r][:], scaled[r][:], ADD)
+            nc.sync.dma_start(out_rows[:, r, :], y01[:, r, :])
+        for q in range(NQ):
+            nc.scalar.copy(yb[q][:, :, 0:2], y01[:, :, q * QW : (q + 1) * QW].rearrange("p r t -> p t r"))
+        for q in range(NQ):
+            cols = slice(q * QW, (q + 1) * QW)
+            nc.gpsimd.tensor_tensor(y23[q][:, 0, :], placed[2][:, cols], scaled[2][:, cols], ADD)
+            nc.sync.dma_start(out_rows[:, 2, cols], y23[q][:, 0, :])
+        for q in range(NQ):
+            cols = slice(q * QW, (q + 1) * QW)
+            nc.vector.scalar_tensor_tensor(y23[q][:, 1, :], od[3][:, cols], OLD_SCALE, placed[3][:, cols], MULT, ADD)
+            nc.sync.dma_start(out_rows[:, 3, cols], y23[q][:, 1, :])
+        words_out = out_1[0].rearrange("p t r -> p (t r)").bitcast(I32)
+        for q in (0, 3, 1, 2):
+            if q < 2:
+                nc.scalar.copy(yb[q][:, :, 2:4], y23[q][:].rearrange("p r t -> p t r"))
+            else:
+                nc.vector.tensor_copy(yb[q][:, :, 2:4], y23[q][:].rearrange("p r t -> p t r"))
+        for q in (0, 3, 1, 2):
+            cols = slice(q * QW, (q + 1) * QW)
+            nc.vector.quantize_mx(out=yq[q][:].bitcast(FP8X4), scales=ys[:, cols], in_=yb[q][:].rearrange("p t r -> p (t r)"))
+            nc.sync.dma_start(words_out[:, cols], yq[q][:].bitcast(I32))
+        for q in range(4):
+            eng = nc.scalar if q % 2 else nc.sync
+            eng.dma_start(out_2[0, 4 * q : 4 * q + 4, :].bitcast(I32), ys[32 * q : 32 * q + 4, :].bitcast(I32))

@@ -38,17 +38,19 @@ def tile_list_read_write_page_pl_kernel(tc, page, wp_words, wp_scales, xt_words,
         read_list = lists.tile([P, J // PER_COL], U16, name="read_list")
         write_list = lists.tile([P, J // PER_COL], U16, name="write_list")
 
-        sc_raw = sb.tile([P, N + J], U8, name="sc_raw", align_bytes=64)
-        nc.gpsimd.memset(sc_raw[:].bitcast(U32), 0)
-        w_sc_raw = sc_raw[:, 0:N]
+        wp_sc_raw = sb.tile([P, N], U8, name="wp_sc_raw", align_bytes=64)
+        wx_sc_raw = sb.tile([P, N], U8, name="wx_sc_raw", align_bytes=64)
+        xt_sc = sb.tile([P, J], U8, name="xt_sc", align_bytes=64)
 
         page_rows = page.rearrange("(p r) t -> p r t", r=PACK)
         old_rows = old.rearrange("(p r) t -> p r t", r=PACK)
         out_rows = out_0.rearrange("(p r) t -> p r t", r=PACK)
 
-        def load_scales(eng, src, q, row0, col0):
-            eng.dma_start(sc_raw[32 * q + row0 : 32 * q + row0 + 4, col0 : col0 + N].bitcast(I32),
-                          src[0, 4 * q : 4 * q + 4, :].bitcast(I32))
+        def load_scales(eng, src, q, dst, copies):
+            rows = src[0, 4 * q : 4 * q + 4, :].bitcast(I32)
+            if copies > 1:
+                rows = rows.unsqueeze(0).to_broadcast([copies, 4, N // 4])
+            eng.dma_start(dst[32 * q : 32 * q + 4 * copies, :].bitcast(I32), rows)
 
         pg = [sb.tile([P, T], F32, name="pg%d" % r) for r in range(PACK)]
         wp_raw = sb.tile([P, N], I32, name="wp_raw", align_bytes=64)
@@ -56,20 +58,19 @@ def tile_list_read_write_page_pl_kernel(tc, page, wp_words, wp_scales, xt_words,
         xt_codes = sb.tile([P, 2 * J], U8, name="xt_codes", align_bytes=64)
         nc.sync.dma_start(read_list[:], offs)
         nc.sync.dma_start(pg[0][:], page_rows[:, 0, :])
-        for q in range(3):
-            load_scales(nc.sync, wp_scales, q, 4, 0)
+        for q in range(4):
+            load_scales(nc.sync, wp_scales, q, wp_sc_raw, 8)
         for r in range(1, PACK):
             nc.sync.dma_start(pg[r][:], page_rows[:, r, :])
         for q in range(4):
-            load_scales(nc.sync, wx_scales, q, 0, 0)
-        load_scales(nc.gpsimd, wp_scales, 3, 4, 0)
+            load_scales(nc.sync, wx_scales, q, wx_sc_raw, 8)
         for q in range(4):
-            load_scales(nc.gpsimd, xt_scales, q, 0, N)
+            load_scales(nc.gpsimd, xt_scales, q, xt_sc, 1)
         nc.sync.dma_start(wp_raw[:], wp_words[0].rearrange("p n t -> p (n t)").bitcast(I32))
         nc.sync.dma_start(wx_raw[:], wx_words[0].rearrange("p n t -> p (n t)").bitcast(I32))
         nc.sync.dma_start(xt_codes[:].bitcast(I32), xt_words[0].bitcast(I32))
         nc.sync.dma_start(write_list[:], offs2)
-        od = [sb.tile([P, T], F32, name="od%d" % r) for r in range(PACK)]
+        od = [sb.tile([P, T], F32, name="od%d" % r, tag="od%d" % r) for r in range(PACK)]
         for r in range(PACK):
             nc.sync.dma_start(od[r][:], old_rows[:, r, :])
 
@@ -98,55 +99,57 @@ def tile_list_read_write_page_pl_kernel(tc, page, wp_words, wp_scales, xt_words,
         for c in range(NCH):
             nc.scalar.copy(xb[c][:, :, 2:4], g23[c][:].rearrange("p r j -> p j r"))
 
-        w_sc = sb.tile([P, PACK, P], U8, name="w_sc", align_bytes=64)
+        wp_sc = sb.tile([P, PACK, P], U8, name="wp_sc", align_bytes=64)
+        wx_sc = sb.tile([P, PACK, P], U8, name="wx_sc", align_bytes=64)
         wp_codes = sb.tile([P, PACK, P], I32, name="wp_codes", align_bytes=64)
         wx_codes = sb.tile([P, PACK, P], I32, name="wx_codes", align_bytes=64)
-        nc.vector.tensor_copy(w_sc[:], w_sc_raw.rearrange("p (m r) -> p r m", r=PACK))
-        nc.vector.tensor_copy(wp_codes[:], wp_raw[:].rearrange("p (m r) -> p r m", r=PACK))
-        nc.vector.tensor_copy(wx_codes[:], wx_raw[:].rearrange("p (m r) -> p r m", r=PACK))
+        nc.vector.tensor_copy(wp_sc[:], wp_sc_raw[:].rearrange("p (m r) -> p r m", r=PACK))
+        nc.vector.tensor_copy(wx_sc[:], wx_sc_raw[:].rearrange("p (m r) -> p r m", r=PACK))
+        nc.vector.tensor_copy(wp_codes[:].rearrange("p r m -> p m r"), wp_raw[:].rearrange("p (m r) -> p m r", r=PACK))
+        nc.vector.tensor_copy(wx_codes[:].rearrange("p r m -> p m r"), wx_raw[:].rearrange("p (m r) -> p m r", r=PACK))
 
         xq = [sb.tile([P, CH], U32, name="xq%d" % c, align_bytes=64) for c in range(NCH)]
         xs = [sb.tile([P, CH], U8, name="xs%d" % c, align_bytes=64) for c in range(NCH)]
         for c in range(NCH):
             nc.vector.quantize_mx(out=xq[c][:].bitcast(FP8X4), scales=xs[c][:], in_=xb[c][:].rearrange("p j r -> p (j r)"))
 
-        h = [sb.tile([P, J], F32, name="h%d" % r) for r in range(PACK)]
-
-        def product(r, c):
-            z = psum.tile([P, CH], F32, name="z%d_%d" % (r, c))
-            nc.tensor.matmul_mx(out=z[:], lhsT=wp_codes[:, r, :].bitcast(FP8X4), lhsT_scale=w_sc[4:P, r, :],
+        def product(r, c, dst):
+            z = psum.tile([P, CH], F32, name="z", bufs=2)
+            nc.tensor.matmul_mx(out=z[:], lhsT=wp_codes[:, r, :].bitcast(FP8X4), lhsT_scale=wp_sc[:, r, :],
                                 rhs=xq[c][:].bitcast(FP8X4), rhs_scale=xs[c][:], start=True, stop=False)
             for u in range(CH // P):
                 j0 = c * CH + u * P
                 nc.tensor.matmul_mx(out=z[:, u * P : (u + 1) * P], lhsT=wx_codes[:, r, :].bitcast(FP8X4),
-                                    lhsT_scale=w_sc[:, r, :], rhs=xt_codes[:, 2 * j0 : 2 * (j0 + P)].bitcast(FP4X4),
-                                    rhs_scale=sc_raw[:, N + j0 : N + j0 + P], start=False, stop=(u == CH // P - 1))
-            nc.scalar.activation(h[r][:, c * CH : (c + 1) * CH], z[:], TANH)
+                                    lhsT_scale=wx_sc[:, r, :], rhs=xt_codes[:, 2 * j0 : 2 * (j0 + P)].bitcast(FP4X4),
+                                    rhs_scale=xt_sc[:, j0 : j0 + P], start=False, stop=(u == CH // P - 1))
+            nc.scalar.activation(dst, z[:], TANH)
 
-        for r, c in ((0, 0), (1, 0), (0, 1), (1, 1)):
-            product(r, c)
-            nc.vector.tensor_copy(placed[r][:].indirect(entries(write_list, c)), h[r][:, c * CH : (c + 1) * CH])
-        for r in (2, 3):
-            for c in range(NCH):
-                product(r, c)
-            nc.vector.tensor_copy(placed[r][:].indirect(write_list[:]), h[r][:])
-
-        scaled = [sb.tile([P, T], F32, name="scaled%d" % r) for r in range(3)]
         y01 = sb.tile([P, 2, T], F32, name="y01")
         y23 = [sb.tile([P, 2, QW], F32, name="y23_%d" % q) for q in range(NQ)]
         yb = [sb.tile([P, QW, PACK], BF16, name="yb%d" % q, align_bytes=64) for q in range(NQ)]
         yq = [sb.tile([P, QW], U32, name="yq%d" % q, align_bytes=64) for q in range(NQ)]
         ys = sb.tile([P, T], U8, name="ys", align_bytes=64)
-        for r in range(3):
-            nc.gpsimd.tensor_scalar(scaled[r][:], od[r][:], OLD_SCALE, 0.0, MULT, ADD)
+
+        for r, c in ((0, 0), (1, 0), (0, 1), (1, 1), (2, 0)):
+            h = sb.tile([P, CH], F32, name="h%d_%d" % (r, c))
+            product(r, c, h[:])
+            nc.vector.tensor_copy(placed[r][:].indirect(entries(write_list, c)), h[:])
         for r in range(2):
-            nc.gpsimd.tensor_tensor(y01[:, r, :], placed[r][:], scaled[r][:], ADD)
+            nc.vector.scalar_tensor_tensor(y01[:, r, :], od[r][:], OLD_SCALE, placed[r][:], MULT, ADD)
             nc.sync.dma_start(out_rows[:, r, :], y01[:, r, :])
+        h = sb.tile([P, CH], F32, name="h2_1", tag="od0")
+        product(2, 1, h[:])
+        nc.vector.tensor_copy(placed[2][:].indirect(entries(write_list, 1)), h[:])
+        h = sb.tile([P, J], F32, name="h3", tag="od1")
+        for c in range(NCH):
+            product(3, c, h[:, c * CH : (c + 1) * CH])
+        nc.vector.tensor_copy(placed[3][:].indirect(write_list[:]), h[:])
+
         for q in range(NQ):
             nc.scalar.copy(yb[q][:, :, 0:2], y01[:, :, q * QW : (q + 1) * QW].rearrange("p r t -> p t r"))
         for q in range(NQ):
             cols = slice(q * QW, (q + 1) * QW)
-            nc.gpsimd.tensor_tensor(y23[q][:, 0, :], placed[2][:, cols], scaled[2][:, cols], ADD)
+            nc.vector.scalar_tensor_tensor(y23[q][:, 0, :], od[2][:, cols], OLD_SCALE, placed[2][:, cols], MULT, ADD)
             nc.sync.dma_start(out_rows[:, 2, cols], y23[q][:, 0, :])
         for q in range(NQ):
             cols = slice(q * QW, (q + 1) * QW)

@@ -16,6 +16,7 @@ FP4X4 = mybir.dt.float4_e2m1fn_x4
 MULT = mybir.AluOpType.mult
 ADD = mybir.AluOpType.add
 TANH = mybir.ActivationFunctionType.Tanh
+COPY = mybir.ActivationFunctionType.Copy
 
 P = 128
 PACK = 4
@@ -53,8 +54,8 @@ def tile_list_read_write_page_pl_kernel(tc, page, wp_words, wp_scales, xt_words,
             eng.dma_start(dst[32 * q : 32 * q + 4 * copies, :].bitcast(I32), rows)
 
         pg = [sb.tile([P, T], F32, name="pg%d" % r) for r in range(PACK)]
-        wp_raw = sb.tile([P, N], I32, name="wp_raw", align_bytes=64)
-        wx_raw = sb.tile([P, N], I32, name="wx_raw", align_bytes=64)
+        wp_raw = sb.tile([P, N], I32, name="wp_raw", tag="wp_raw", align_bytes=64)
+        wx_raw = sb.tile([P, N], I32, name="wx_raw", tag="wx_raw", align_bytes=64)
         xt_codes = sb.tile([P, 2 * J], U8, name="xt_codes", align_bytes=64)
         nc.sync.dma_start(read_list[:], offs)
         nc.sync.dma_start(pg[0][:], page_rows[:, 0, :])
@@ -63,9 +64,9 @@ def tile_list_read_write_page_pl_kernel(tc, page, wp_words, wp_scales, xt_words,
         for r in range(1, PACK):
             nc.sync.dma_start(pg[r][:], page_rows[:, r, :])
         for q in range(4):
-            load_scales(nc.sync, wx_scales, q, wx_sc_raw, 8)
+            load_scales(nc.sync, xt_scales, q, xt_sc, 1)
         for q in range(4):
-            load_scales(nc.gpsimd, xt_scales, q, xt_sc, 1)
+            load_scales(nc.gpsimd, wx_scales, q, wx_sc_raw, 8)
         nc.sync.dma_start(wp_raw[:], wp_words[0].rearrange("p n t -> p (n t)").bitcast(I32))
         nc.sync.dma_start(wx_raw[:], wx_words[0].rearrange("p n t -> p (n t)").bitcast(I32))
         nc.sync.dma_start(xt_codes[:].bitcast(I32), xt_words[0].bitcast(I32))
@@ -79,16 +80,16 @@ def tile_list_read_write_page_pl_kernel(tc, page, wp_words, wp_scales, xt_words,
         nc.vector.memset(warm[:], 0.0)
         nc.scalar.activation(warm_out[:], warm[:], TANH)
 
-        placed = [sb.tile([P, T], F32, name="placed%d" % r) for r in range(PACK)]
-        for r in range(PACK):
-            (nc.vector if r < 2 else nc.gpsimd).memset(placed[r][:], 0.0)
+        placed = [sb.tile([P, T], F32, name="placed%d" % r) for r in range(2)]
+        for r in range(2):
+            nc.vector.memset(placed[r][:], 0.0)
 
         def entries(lst, c):
             return lst[:, c * CH // PER_COL : (c + 1) * CH // PER_COL]
 
         g01 = sb.tile([P, 2, J], F32, name="g01")
         g23 = [sb.tile([P, 2, CH], F32, name="g23_%d" % c) for c in range(NCH)]
-        xb = [sb.tile([P, CH, PACK], BF16, name="xb%d" % c, align_bytes=64) for c in range(NCH)]
+        xb = [sb.tile([P, CH, PACK], BF16, name="xb%d" % c, tag="xb%d" % c, align_bytes=64) for c in range(NCH)]
         for r in range(2):
             nc.vector.tensor_copy(g01[:, r, :], pg[r][:].indirect(read_list[:]))
         for c in range(NCH):
@@ -101,22 +102,29 @@ def tile_list_read_write_page_pl_kernel(tc, page, wp_words, wp_scales, xt_words,
 
         wp_sc = sb.tile([P, PACK, P], U8, name="wp_sc", align_bytes=64)
         wx_sc = sb.tile([P, PACK, P], U8, name="wx_sc", align_bytes=64)
+        nc.gpsimd.tensor_copy(wp_sc[:], wp_sc_raw[:].rearrange("p (m r) -> p r m", r=PACK))
+        nc.gpsimd.tensor_copy(wx_sc[:], wx_sc_raw[:].rearrange("p (m r) -> p r m", r=PACK))
+
         wp_codes = sb.tile([P, PACK, P], I32, name="wp_codes", align_bytes=64)
         wx_codes = sb.tile([P, PACK, P], I32, name="wx_codes", align_bytes=64)
-        nc.vector.tensor_copy(wp_sc[:], wp_sc_raw[:].rearrange("p (m r) -> p r m", r=PACK))
-        nc.vector.tensor_copy(wx_sc[:], wx_sc_raw[:].rearrange("p (m r) -> p r m", r=PACK))
-        nc.vector.tensor_copy(wp_codes[:].rearrange("p r m -> p m r"), wp_raw[:].rearrange("p (m r) -> p m r", r=PACK))
-        nc.vector.tensor_copy(wx_codes[:].rearrange("p r m -> p m r"), wx_raw[:].rearrange("p (m r) -> p m r", r=PACK))
+        for codes, raw in ((wp_codes, wp_raw), (wx_codes, wx_raw)):
+            nc.vector.tensor_copy(codes[:].rearrange("p r m -> p m r"), raw[:].rearrange("p (m r) -> p m r", r=PACK))
 
-        xq = [sb.tile([P, CH], U32, name="xq%d" % c, align_bytes=64) for c in range(NCH)]
-        xs = [sb.tile([P, CH], U8, name="xs%d" % c, align_bytes=64) for c in range(NCH)]
+        xq = sb.tile([P, J], U32, name="xq", tag="wp_raw", align_bytes=64)
+        xs = sb.tile([P, J], U8, name="xs", tag="wx_raw", align_bytes=64)
         for c in range(NCH):
-            nc.vector.quantize_mx(out=xq[c][:].bitcast(FP8X4), scales=xs[c][:], in_=xb[c][:].rearrange("p j r -> p (j r)"))
+            cols = slice(c * CH, (c + 1) * CH)
+            nc.vector.quantize_mx(out=xq[:, cols].bitcast(FP8X4), scales=xs[:, cols], in_=xb[c][:].rearrange("p j r -> p (j r)"))
+
+        for r in (2, 3):
+            late = sb.tile([P, T], F32, name="placed%d" % r, tag="xb%d" % (r - 2), align_bytes=64)
+            nc.gpsimd.memset(late[:], 0.0)
+            placed.append(late)
 
         def product(r, c, dst):
             z = psum.tile([P, CH], F32, name="z", bufs=2)
             nc.tensor.matmul_mx(out=z[:], lhsT=wp_codes[:, r, :].bitcast(FP8X4), lhsT_scale=wp_sc[:, r, :],
-                                rhs=xq[c][:].bitcast(FP8X4), rhs_scale=xs[c][:], start=True, stop=False)
+                                rhs=xq[:, c * CH : (c + 1) * CH].bitcast(FP8X4), rhs_scale=xs[:, c * CH : (c + 1) * CH], start=True, stop=False)
             for u in range(CH // P):
                 j0 = c * CH + u * P
                 nc.tensor.matmul_mx(out=z[:, u * P : (u + 1) * P], lhsT=wx_codes[:, r, :].bitcast(FP8X4),
@@ -124,47 +132,57 @@ def tile_list_read_write_page_pl_kernel(tc, page, wp_words, wp_scales, xt_words,
                                     rhs_scale=xt_sc[:, j0 : j0 + P], start=False, stop=(u == CH // P - 1))
             nc.scalar.activation(dst, z[:], TANH)
 
-        y01 = sb.tile([P, 2, T], F32, name="y01")
+        y01 = [sb.tile([P, 2, 2 * QW], F32, name="y01_%d" % u) for u in range(2)]
         y23 = [sb.tile([P, 2, QW], F32, name="y23_%d" % q) for q in range(NQ)]
         yb = [sb.tile([P, QW, PACK], BF16, name="yb%d" % q, align_bytes=64) for q in range(NQ)]
         yq = [sb.tile([P, QW], U32, name="yq%d" % q, align_bytes=64) for q in range(NQ)]
         ys = sb.tile([P, T], U8, name="ys", align_bytes=64)
 
-        for r, c in ((0, 0), (1, 0), (0, 1), (1, 1), (2, 0)):
+        for r, c in ((0, 0), (1, 0), (0, 1), (1, 1)):
             h = sb.tile([P, CH], F32, name="h%d_%d" % (r, c))
             product(r, c, h[:])
             nc.vector.tensor_copy(placed[r][:].indirect(entries(write_list, c)), h[:])
-        for r in range(2):
-            nc.vector.scalar_tensor_tensor(y01[:, r, :], od[r][:], OLD_SCALE, placed[r][:], MULT, ADD)
-            nc.sync.dma_start(out_rows[:, r, :], y01[:, r, :])
-        h = sb.tile([P, CH], F32, name="h2_1", tag="od0")
-        product(2, 1, h[:])
-        nc.vector.tensor_copy(placed[2][:].indirect(entries(write_list, 1)), h[:])
-        h = sb.tile([P, J], F32, name="h3", tag="od1")
-        for c in range(NCH):
-            product(3, c, h[:, c * CH : (c + 1) * CH])
-        nc.vector.tensor_copy(placed[3][:].indirect(write_list[:]), h[:])
+        for r in (2, 3):
+            h = sb.tile([P, J], F32, name="h%d" % r)
+            for c in range(NCH):
+                product(r, c, h[:, c * CH : (c + 1) * CH])
+            nc.vector.tensor_copy(placed[r][:].indirect(write_list[:]), h[:])
 
+        scaled = []
+        for r, tag in enumerate(("wp_raw", "wx_raw")):
+            s = sb.tile([P, T], F32, name="scaled%d" % r, tag=tag, align_bytes=64)
+            nc.scalar.activation(s[:], od[r][:], COPY, scale=OLD_SCALE)
+            scaled.append(s)
         for q in range(NQ):
-            nc.scalar.copy(yb[q][:, :, 0:2], y01[:, :, q * QW : (q + 1) * QW].rearrange("p r t -> p t r"))
+            nc.scalar.activation(y23[q][:, 1, :], od[2][:, q * QW : (q + 1) * QW], COPY, scale=OLD_SCALE)
+        for r in range(2):
+            for u in range(2):
+                cols = slice(2 * u * QW, 2 * (u + 1) * QW)
+                nc.gpsimd.tensor_tensor(y01[u][:, r, :], placed[r][:, cols], scaled[r][:, cols], ADD)
+                nc.sync.dma_start(out_rows[:, r, cols], y01[u][:, r, :])
+        for q in range(NQ):
+            nc.scalar.copy(yb[q][:, :, 0:2], y01[q // 2][:, :, (q % 2) * QW : (q % 2 + 1) * QW].rearrange("p r t -> p t r"))
         for q in range(NQ):
             cols = slice(q * QW, (q + 1) * QW)
-            nc.vector.scalar_tensor_tensor(y23[q][:, 0, :], od[2][:, cols], OLD_SCALE, placed[2][:, cols], MULT, ADD)
+            nc.gpsimd.tensor_tensor(y23[q][:, 0, :], placed[2][:, cols], y23[q][:, 1, :], ADD)
             nc.sync.dma_start(out_rows[:, 2, cols], y23[q][:, 0, :])
         for q in range(NQ):
             cols = slice(q * QW, (q + 1) * QW)
             nc.vector.scalar_tensor_tensor(y23[q][:, 1, :], od[3][:, cols], OLD_SCALE, placed[3][:, cols], MULT, ADD)
             nc.sync.dma_start(out_rows[:, 3, cols], y23[q][:, 1, :])
         words_out = out_1[0].rearrange("p t r -> p (t r)").bitcast(I32)
-        for q in (0, 3, 1, 2):
-            if q < 2:
-                nc.scalar.copy(yb[q][:, :, 2:4], y23[q][:].rearrange("p r t -> p t r"))
-            else:
-                nc.vector.tensor_copy(yb[q][:, :, 2:4], y23[q][:].rearrange("p r t -> p t r"))
-        for q in (0, 3, 1, 2):
+
+        def quantise_result(q):
             cols = slice(q * QW, (q + 1) * QW)
             nc.vector.quantize_mx(out=yq[q][:].bitcast(FP8X4), scales=ys[:, cols], in_=yb[q][:].rearrange("p t r -> p (t r)"))
             nc.sync.dma_start(words_out[:, cols], yq[q][:].bitcast(I32))
+
+        for q in range(NQ - 1):
+            nc.scalar.copy(yb[q][:, :, 2:4], y23[q][:].rearrange("p r t -> p t r"))
+        quantise_result(0)
+        nc.vector.tensor_copy(yb[3][:, :, 2:4], y23[3][:].rearrange("p r t -> p t r"))
+        for q in (1, 3, 2):
+            quantise_result(q)
         for q in range(4):
             eng = nc.scalar if q % 2 else nc.sync
             eng.dma_start(out_2[0, 4 * q : 4 * q + 4, :].bitcast(I32), ys[32 * q : 32 * q + 4, :].bitcast(I32))

@@ -20,11 +20,15 @@ COPY = mybir.ActivationFunctionType.Copy
 
 P = 128
 PACK = 4
+QUADS = 4
+QUAD = P // QUADS
+QUAD_ROWS = 4
 PER_COL = 16
-CH = 256
-NCH = J // CH
-QW = 256
-NQ = T // QW
+CHUNK = 256
+CHUNKS = J // CHUNK
+PART = 256
+PARTS = T // PART
+Z_BANKS = 2
 OLD_SCALE = 0.3
 
 
@@ -47,58 +51,55 @@ def tile_list_read_write_page_pl_kernel(tc, page, wp_words, wp_scales, xt_words,
         old_rows = old.rearrange("(p r) t -> p r t", r=PACK)
         out_rows = out_0.rearrange("(p r) t -> p r t", r=PACK)
 
-        def load_scales(eng, src, q, dst, copies):
-            rows = src[0, 4 * q : 4 * q + 4, :].bitcast(I32)
-            if copies > 1:
-                rows = rows.unsqueeze(0).to_broadcast([copies, 4, N // 4])
-            eng.dma_start(dst[32 * q : 32 * q + 4 * copies, :].bitcast(I32), rows)
+        def scale_rows(scales, q):
+            return scales[0, QUAD_ROWS * q : QUAD_ROWS * (q + 1), :].bitcast(I32)
 
-        pg = [sb.tile([P, T], F32, name="pg%d" % r) for r in range(PACK)]
+        def load_scales_to_deal(eng, scales, dst):
+            for q in range(QUADS):
+                rows = scale_rows(scales, q).unsqueeze(0).to_broadcast([QUAD // QUAD_ROWS, QUAD_ROWS, N // 4])
+                eng.dma_start(dst[QUAD * q : QUAD * (q + 1), :].bitcast(I32), rows)
+
+        page_sb = [sb.tile([P, T], F32, name="page%d" % r) for r in range(PACK)]
         wp_raw = sb.tile([P, N], I32, name="wp_raw", tag="wp_raw", align_bytes=64)
         wx_raw = sb.tile([P, N], I32, name="wx_raw", tag="wx_raw", align_bytes=64)
         xt_codes = sb.tile([P, 2 * J], U8, name="xt_codes", align_bytes=64)
         nc.sync.dma_start(read_list[:], offs)
-        nc.sync.dma_start(pg[0][:], page_rows[:, 0, :])
-        for q in range(4):
-            load_scales(nc.sync, wp_scales, q, wp_sc_raw, 8)
+        nc.sync.dma_start(page_sb[0][:], page_rows[:, 0, :])
+        load_scales_to_deal(nc.sync, wp_scales, wp_sc_raw)
         for r in range(1, PACK):
-            nc.sync.dma_start(pg[r][:], page_rows[:, r, :])
-        for q in range(4):
-            load_scales(nc.sync, xt_scales, q, xt_sc, 1)
-        for q in range(4):
-            load_scales(nc.gpsimd, wx_scales, q, wx_sc_raw, 8)
-        nc.sync.dma_start(wp_raw[:], wp_words[0].rearrange("p n t -> p (n t)").bitcast(I32))
+            nc.sync.dma_start(page_sb[r][:], page_rows[:, r, :])
+        for q in range(QUADS):
+            nc.sync.dma_start(xt_sc[QUAD * q : QUAD * q + QUAD_ROWS, :].bitcast(I32), scale_rows(xt_scales, q))
+        load_scales_to_deal(nc.gpsimd, wx_scales, wx_sc_raw)
         nc.sync.dma_start(wx_raw[:], wx_words[0].rearrange("p n t -> p (n t)").bitcast(I32))
         nc.sync.dma_start(xt_codes[:].bitcast(I32), xt_words[0].bitcast(I32))
+        nc.sync.dma_start(wp_raw[:], wp_words[0].rearrange("p n t -> p (n t)").bitcast(I32))
         nc.sync.dma_start(write_list[:], offs2)
-        od = [sb.tile([P, T], F32, name="od%d" % r, tag="od%d" % r) for r in range(PACK)]
+        old_sb = [sb.tile([P, T], F32, name="old%d" % r) for r in range(PACK)]
         for r in range(PACK):
-            nc.sync.dma_start(od[r][:], old_rows[:, r, :])
-
-        warm = sb.tile([P, 8], F32, name="warm")
-        warm_out = sb.tile([P, 8], F32, name="warm_out")
-        nc.vector.memset(warm[:], 0.0)
-        nc.scalar.activation(warm_out[:], warm[:], TANH)
+            nc.sync.dma_start(old_sb[r][:], old_rows[:, r, :])
 
         placed = [sb.tile([P, T], F32, name="placed%d" % r) for r in range(2)]
         for r in range(2):
             nc.vector.memset(placed[r][:], 0.0)
 
         def entries(lst, c):
-            return lst[:, c * CH // PER_COL : (c + 1) * CH // PER_COL]
+            return lst[:, c * CHUNK // PER_COL : (c + 1) * CHUNK // PER_COL]
 
-        g01 = sb.tile([P, 2, J], F32, name="g01")
-        g23 = [sb.tile([P, 2, CH], F32, name="g23_%d" % c) for c in range(NCH)]
-        xb = [sb.tile([P, CH, PACK], BF16, name="xb%d" % c, tag="xb%d" % c, align_bytes=64) for c in range(NCH)]
+        picked01 = sb.tile([P, 2, J], F32, name="picked01")
+        picked23 = [sb.tile([P, 2, CHUNK], F32, name="picked23_%d" % c) for c in range(CHUNKS)]
+        picked_bf = [sb.tile([P, CHUNK, PACK], BF16, name="picked_bf%d" % c, tag="picked_bf%d" % c, align_bytes=64)
+                     for c in range(CHUNKS)]
         for r in range(2):
-            nc.vector.tensor_copy(g01[:, r, :], pg[r][:].indirect(read_list[:]))
-        for c in range(NCH):
-            nc.scalar.copy(xb[c][:, :, 0:2], g01[:, :, c * CH : (c + 1) * CH].rearrange("p r j -> p j r"))
+            nc.vector.tensor_copy(picked01[:, r, :], page_sb[r][:].indirect(read_list[:]))
+        for c in range(CHUNKS):
+            nc.scalar.activation(picked_bf[c][:, :, 0:2],
+                                 picked01[:, :, c * CHUNK : (c + 1) * CHUNK].rearrange("p r j -> p j r"), COPY)
         for r in range(2, PACK):
-            for c in range(NCH):
-                nc.vector.tensor_copy(g23[c][:, r - 2, :], pg[r][:].indirect(entries(read_list, c)))
-        for c in range(NCH):
-            nc.scalar.copy(xb[c][:, :, 2:4], g23[c][:].rearrange("p r j -> p j r"))
+            for c in range(CHUNKS):
+                nc.vector.tensor_copy(picked23[c][:, r - 2, :], page_sb[r][:].indirect(entries(read_list, c)))
+        for c in range(CHUNKS):
+            nc.scalar.copy(picked_bf[c][:, :, 2:4], picked23[c][:].rearrange("p r j -> p j r"))
 
         wp_sc = sb.tile([P, PACK, P], U8, name="wp_sc", align_bytes=64)
         wx_sc = sb.tile([P, PACK, P], U8, name="wx_sc", align_bytes=64)
@@ -107,82 +108,90 @@ def tile_list_read_write_page_pl_kernel(tc, page, wp_words, wp_scales, xt_words,
 
         wp_codes = sb.tile([P, PACK, P], I32, name="wp_codes", align_bytes=64)
         wx_codes = sb.tile([P, PACK, P], I32, name="wx_codes", align_bytes=64)
-        for codes, raw in ((wp_codes, wp_raw), (wx_codes, wx_raw)):
+        for codes, raw in ((wx_codes, wx_raw), (wp_codes, wp_raw)):
             nc.vector.tensor_copy(codes[:].rearrange("p r m -> p m r"), raw[:].rearrange("p (m r) -> p m r", r=PACK))
 
-        xq = sb.tile([P, J], U32, name="xq", tag="wp_raw", align_bytes=64)
-        xs = sb.tile([P, J], U8, name="xs", tag="wx_raw", align_bytes=64)
-        for c in range(NCH):
-            cols = slice(c * CH, (c + 1) * CH)
-            nc.vector.quantize_mx(out=xq[:, cols].bitcast(FP8X4), scales=xs[:, cols], in_=xb[c][:].rearrange("p j r -> p (j r)"))
+        picked_codes = sb.tile([P, J], U32, name="picked_codes", tag="wp_raw", align_bytes=64)
+        picked_sc = sb.tile([P, J], U8, name="picked_sc", tag="wx_raw", align_bytes=64)
+        for c in range(CHUNKS):
+            cols = slice(c * CHUNK, (c + 1) * CHUNK)
+            nc.vector.quantize_mx(out=picked_codes[:, cols].bitcast(FP8X4), scales=picked_sc[:, cols],
+                                  in_=picked_bf[c][:].rearrange("p j r -> p (j r)"))
 
         for r in (2, 3):
-            late = sb.tile([P, T], F32, name="placed%d" % r, tag="xb%d" % (r - 2), align_bytes=64)
+            late = sb.tile([P, T], F32, name="placed%d" % r, tag="picked_bf%d" % (r - 2), align_bytes=64)
             nc.gpsimd.memset(late[:], 0.0)
             placed.append(late)
 
         def product(r, c, dst):
-            z = psum.tile([P, CH], F32, name="z", bufs=2)
-            nc.tensor.matmul_mx(out=z[:], lhsT=wp_codes[:, r, :].bitcast(FP8X4), lhsT_scale=wp_sc[:, r, :],
-                                rhs=xq[:, c * CH : (c + 1) * CH].bitcast(FP8X4), rhs_scale=xs[:, c * CH : (c + 1) * CH], start=True, stop=False)
-            for u in range(CH // P):
-                j0 = c * CH + u * P
+            z = psum.tile([P, CHUNK], F32, name="z", bufs=Z_BANKS)
+            for u in range(CHUNK // P):
+                j0 = c * CHUNK + u * P
                 nc.tensor.matmul_mx(out=z[:, u * P : (u + 1) * P], lhsT=wx_codes[:, r, :].bitcast(FP8X4),
                                     lhsT_scale=wx_sc[:, r, :], rhs=xt_codes[:, 2 * j0 : 2 * (j0 + P)].bitcast(FP4X4),
-                                    rhs_scale=xt_sc[:, j0 : j0 + P], start=False, stop=(u == CH // P - 1))
+                                    rhs_scale=xt_sc[:, j0 : j0 + P], start=(u == 0), stop=False)
+            slots = slice(c * CHUNK, (c + 1) * CHUNK)
+            nc.tensor.matmul_mx(out=z[:], lhsT=wp_codes[:, r, :].bitcast(FP8X4), lhsT_scale=wp_sc[:, r, :],
+                                rhs=picked_codes[:, slots].bitcast(FP8X4), rhs_scale=picked_sc[:, slots],
+                                start=False, stop=True)
             nc.scalar.activation(dst, z[:], TANH)
 
-        y01 = [sb.tile([P, 2, 2 * QW], F32, name="y01_%d" % u) for u in range(2)]
-        y23 = [sb.tile([P, 2, QW], F32, name="y23_%d" % q) for q in range(NQ)]
-        yb = [sb.tile([P, QW, PACK], BF16, name="yb%d" % q, align_bytes=64) for q in range(NQ)]
-        yq = [sb.tile([P, QW], U32, name="yq%d" % q, align_bytes=64) for q in range(NQ)]
-        ys = sb.tile([P, T], U8, name="ys", align_bytes=64)
+        y01 = [sb.tile([P, 2, 2 * PART], F32, name="y01_%d" % u) for u in range(PARTS // 2)]
+        y23 = [sb.tile([P, 2, PART], F32, name="y23_%d" % a) for a in range(PARTS)]
+        y_bf = [sb.tile([P, PART, PACK], BF16, name="y_bf%d" % a, align_bytes=64) for a in range(PARTS)]
+        y_codes = [sb.tile([P, PART], U32, name="y_codes%d" % a, align_bytes=64) for a in range(PARTS)]
+        y_sc = sb.tile([P, T], U8, name="y_sc", align_bytes=64)
 
-        for r, c in ((0, 0), (1, 0), (0, 1), (1, 1)):
-            h = sb.tile([P, CH], F32, name="h%d_%d" % (r, c))
-            product(r, c, h[:])
-            nc.vector.tensor_copy(placed[r][:].indirect(entries(write_list, c)), h[:])
+        for c in range(CHUNKS):
+            for r in range(2):
+                h = sb.tile([P, CHUNK], F32, name="h%d_%d" % (r, c))
+                product(r, c, h[:])
+                nc.vector.tensor_copy(placed[r][:].indirect(entries(write_list, c)), h[:])
         for r in (2, 3):
             h = sb.tile([P, J], F32, name="h%d" % r)
-            for c in range(NCH):
-                product(r, c, h[:, c * CH : (c + 1) * CH])
+            for c in range(CHUNKS):
+                product(r, c, h[:, c * CHUNK : (c + 1) * CHUNK])
             nc.vector.tensor_copy(placed[r][:].indirect(write_list[:]), h[:])
 
         scaled = []
         for r, tag in enumerate(("wp_raw", "wx_raw")):
-            s = sb.tile([P, T], F32, name="scaled%d" % r, tag=tag, align_bytes=64)
-            nc.scalar.activation(s[:], od[r][:], COPY, scale=OLD_SCALE)
-            scaled.append(s)
-        for q in range(NQ):
-            nc.scalar.activation(y23[q][:, 1, :], od[2][:, q * QW : (q + 1) * QW], COPY, scale=OLD_SCALE)
+            scaled_rows = sb.tile([P, T], F32, name="scaled%d" % r, tag=tag, align_bytes=64)
+            nc.scalar.activation(scaled_rows[:], old_sb[r][:], COPY, scale=OLD_SCALE)
+            scaled.append(scaled_rows)
+        for a in range(PARTS):
+            nc.scalar.activation(y23[a][:, 1, :], old_sb[2][:, a * PART : (a + 1) * PART], COPY, scale=OLD_SCALE)
         for r in range(2):
-            for u in range(2):
-                cols = slice(2 * u * QW, 2 * (u + 1) * QW)
+            for u in range(PARTS // 2):
+                cols = slice(2 * u * PART, 2 * (u + 1) * PART)
                 nc.gpsimd.tensor_tensor(y01[u][:, r, :], placed[r][:, cols], scaled[r][:, cols], ADD)
                 nc.sync.dma_start(out_rows[:, r, cols], y01[u][:, r, :])
-        for q in range(NQ):
-            nc.scalar.copy(yb[q][:, :, 0:2], y01[q // 2][:, :, (q % 2) * QW : (q % 2 + 1) * QW].rearrange("p r t -> p t r"))
-        for q in range(NQ):
-            cols = slice(q * QW, (q + 1) * QW)
-            nc.gpsimd.tensor_tensor(y23[q][:, 0, :], placed[2][:, cols], y23[q][:, 1, :], ADD)
-            nc.sync.dma_start(out_rows[:, 2, cols], y23[q][:, 0, :])
-        for q in range(NQ):
-            cols = slice(q * QW, (q + 1) * QW)
-            nc.vector.scalar_tensor_tensor(y23[q][:, 1, :], od[3][:, cols], OLD_SCALE, placed[3][:, cols], MULT, ADD)
-            nc.sync.dma_start(out_rows[:, 3, cols], y23[q][:, 1, :])
+        for a in range(PARTS):
+            nc.scalar.copy(y_bf[a][:, :, 0:2],
+                           y01[a // 2][:, :, (a % 2) * PART : (a % 2 + 1) * PART].rearrange("p r t -> p t r"))
+        for a in range(PARTS):
+            cols = slice(a * PART, (a + 1) * PART)
+            nc.gpsimd.tensor_tensor(y23[a][:, 0, :], placed[2][:, cols], y23[a][:, 1, :], ADD)
+            nc.sync.dma_start(out_rows[:, 2, cols], y23[a][:, 0, :])
+        for a in range(PARTS):
+            cols = slice(a * PART, (a + 1) * PART)
+            nc.vector.scalar_tensor_tensor(y23[a][:, 1, :], old_sb[3][:, cols], OLD_SCALE, placed[3][:, cols], MULT, ADD)
+            nc.sync.dma_start(out_rows[:, 3, cols], y23[a][:, 1, :])
         words_out = out_1[0].rearrange("p t r -> p (t r)").bitcast(I32)
 
-        def quantise_result(q):
-            cols = slice(q * QW, (q + 1) * QW)
-            nc.vector.quantize_mx(out=yq[q][:].bitcast(FP8X4), scales=ys[:, cols], in_=yb[q][:].rearrange("p t r -> p (t r)"))
-            nc.sync.dma_start(words_out[:, cols], yq[q][:].bitcast(I32))
+        def quantise_result(a):
+            cols = slice(a * PART, (a + 1) * PART)
+            nc.vector.quantize_mx(out=y_codes[a][:].bitcast(FP8X4), scales=y_sc[:, cols],
+                                  in_=y_bf[a][:].rearrange("p t r -> p (t r)"))
+            nc.sync.dma_start(words_out[:, cols], y_codes[a][:].bitcast(I32))
 
-        for q in range(NQ - 1):
-            nc.scalar.copy(yb[q][:, :, 2:4], y23[q][:].rearrange("p r t -> p t r"))
+        last = PARTS - 1
+        for a in range(last):
+            nc.scalar.copy(y_bf[a][:, :, 2:4], y23[a][:].rearrange("p r t -> p t r"))
         quantise_result(0)
-        nc.vector.tensor_copy(yb[3][:, :, 2:4], y23[3][:].rearrange("p r t -> p t r"))
-        for q in (1, 3, 2):
-            quantise_result(q)
-        for q in range(4):
+        nc.vector.tensor_copy(y_bf[last][:, :, 2:4], y23[last][:].rearrange("p r t -> p t r"))
+        for a in (1, last, last - 1):
+            quantise_result(a)
+
+        for q in range(QUADS):
             eng = nc.scalar if q % 2 else nc.sync
-            eng.dma_start(out_2[0, 4 * q : 4 * q + 4, :].bitcast(I32), ys[32 * q : 32 * q + 4, :].bitcast(I32))
+            eng.dma_start(scale_rows(out_2, q), y_sc[QUAD * q : QUAD * q + QUAD_ROWS, :].bitcast(I32))

from contextlib import ExitStack

import concourse.mybir as mybir

K, L, T, J, N = 512, 512, 1024, 512, 512
FLOPS = 2 * N * J * (K + L)

F32 = mybir.dt.float32
BF16 = mybir.dt.bfloat16
I32 = mybir.dt.int32
U32 = mybir.dt.uint32
U16 = mybir.dt.uint16
U8 = mybir.dt.uint8
FP8X4 = mybir.dt.float8_e4m3fn_x4
FP4X4 = mybir.dt.float4_e2m1fn_x4
MULT = mybir.AluOpType.mult
ADD = mybir.AluOpType.add
TANH = mybir.ActivationFunctionType.Tanh
COPY = mybir.ActivationFunctionType.Copy

P = 128
PACK = 4
QUADS = 4
QUAD = P // QUADS
QUAD_ROWS = 4
PER_COL = 16
CHUNK = 256
CHUNKS = J // CHUNK
PART = 256
PARTS = T // PART
Z_BANKS = 2
OLD_SCALE = 0.3


def tile_list_read_write_page_pl_kernel(tc, page, wp_words, wp_scales, xt_words, xt_scales, wx_words, wx_scales,
                                           old, offs, offs2, out_0, out_1, out_2):
    nc = tc.nc
    with ExitStack() as ctx:
        lists = ctx.enter_context(tc.tile_pool(name="lists", bufs=1))
        sb = ctx.enter_context(tc.tile_pool(name="sb", bufs=1))
        psum = ctx.enter_context(tc.psum_pool(name="psum", bufs=1))

        read_list = lists.tile([P, J // PER_COL], U16, name="read_list")
        write_list = lists.tile([P, J // PER_COL], U16, name="write_list")

        wp_sc_raw = sb.tile([P, N], U8, name="wp_sc_raw", align_bytes=64)
        wx_sc_raw = sb.tile([P, N], U8, name="wx_sc_raw", align_bytes=64)
        xt_sc = sb.tile([P, J], U8, name="xt_sc", align_bytes=64)

        page_rows = page.rearrange("(p r) t -> p r t", r=PACK)
        old_rows = old.rearrange("(p r) t -> p r t", r=PACK)
        out_rows = out_0.rearrange("(p r) t -> p r t", r=PACK)

        def scale_rows(scales, q):
            return scales[0, QUAD_ROWS * q : QUAD_ROWS * (q + 1), :].bitcast(I32)

        def load_scales_to_deal(eng, scales, dst):
            for q in range(QUADS):
                rows = scale_rows(scales, q).unsqueeze(0).to_broadcast([QUAD // QUAD_ROWS, QUAD_ROWS, N // 4])
                eng.dma_start(dst[QUAD * q : QUAD * (q + 1), :].bitcast(I32), rows)

        page_sb = [sb.tile([P, T], F32, name="page%d" % r) for r in range(PACK)]
        wp_raw = sb.tile([P, N], I32, name="wp_raw", tag="wp_raw", align_bytes=64)
        wx_raw = sb.tile([P, N], I32, name="wx_raw", tag="wx_raw", align_bytes=64)
        xt_codes = sb.tile([P, 2 * J], U8, name="xt_codes", align_bytes=64)
        nc.sync.dma_start(read_list[:], offs)
        nc.sync.dma_start(page_sb[0][:], page_rows[:, 0, :])
        load_scales_to_deal(nc.sync, wp_scales, wp_sc_raw)
        for r in range(1, PACK):
            nc.sync.dma_start(page_sb[r][:], page_rows[:, r, :])
        for q in range(QUADS):
            nc.sync.dma_start(xt_sc[QUAD * q : QUAD * q + QUAD_ROWS, :].bitcast(I32), scale_rows(xt_scales, q))
        load_scales_to_deal(nc.gpsimd, wx_scales, wx_sc_raw)
        nc.sync.dma_start(wx_raw[:], wx_words[0].rearrange("p n t -> p (n t)").bitcast(I32))
        nc.sync.dma_start(xt_codes[:].bitcast(I32), xt_words[0].bitcast(I32))
        nc.sync.dma_start(wp_raw[:], wp_words[0].rearrange("p n t -> p (n t)").bitcast(I32))
        nc.sync.dma_start(write_list[:], offs2)
        old_sb = [sb.tile([P, T], F32, name="old%d" % r) for r in range(PACK)]
        for r in range(PACK):
            nc.sync.dma_start(old_sb[r][:], old_rows[:, r, :])

        placed = [sb.tile([P, T], F32, name="placed%d" % r) for r in range(2)]
        for r in range(2):
            nc.vector.memset(placed[r][:], 0.0)

        def entries(lst, c):
            return lst[:, c * CHUNK // PER_COL : (c + 1) * CHUNK // PER_COL]

        picked01 = sb.tile([P, 2, J], F32, name="picked01")
        picked23 = [sb.tile([P, 2, CHUNK], F32, name="picked23_%d" % c) for c in range(CHUNKS)]
        picked_bf = [sb.tile([P, CHUNK, PACK], BF16, name="picked_bf%d" % c, tag="picked_bf%d" % c, align_bytes=64)
                     for c in range(CHUNKS)]
        for r in range(2):
            nc.vector.tensor_copy(picked01[:, r, :], page_sb[r][:].indirect(read_list[:]))
        for c in range(CHUNKS):
            nc.scalar.activation(picked_bf[c][:, :, 0:2],
                                 picked01[:, :, c * CHUNK : (c + 1) * CHUNK].rearrange("p r j -> p j r"), COPY)
        for r in range(2, PACK):
            for c in range(CHUNKS):
                nc.vector.tensor_copy(picked23[c][:, r - 2, :], page_sb[r][:].indirect(entries(read_list, c)))
        for c in range(CHUNKS):
            nc.scalar.copy(picked_bf[c][:, :, 2:4], picked23[c][:].rearrange("p r j -> p j r"))

        wp_sc = sb.tile([P, PACK, P], U8, name="wp_sc", align_bytes=64)
        wx_sc = sb.tile([P, PACK, P], U8, name="wx_sc", align_bytes=64)
        nc.gpsimd.tensor_copy(wp_sc[:], wp_sc_raw[:].rearrange("p (m r) -> p r m", r=PACK))
        nc.gpsimd.tensor_copy(wx_sc[:], wx_sc_raw[:].rearrange("p (m r) -> p r m", r=PACK))

        wp_codes = sb.tile([P, PACK, P], I32, name="wp_codes", align_bytes=64)
        wx_codes = sb.tile([P, PACK, P], I32, name="wx_codes", align_bytes=64)
        for codes, raw in ((wx_codes, wx_raw), (wp_codes, wp_raw)):
            nc.vector.tensor_copy(codes[:].rearrange("p r m -> p m r"), raw[:].rearrange("p (m r) -> p m r", r=PACK))

        picked_codes = sb.tile([P, J], U32, name="picked_codes", tag="wp_raw", align_bytes=64)
        picked_sc = sb.tile([P, J], U8, name="picked_sc", tag="wx_raw", align_bytes=64)
        for c in range(CHUNKS):
            cols = slice(c * CHUNK, (c + 1) * CHUNK)
            nc.vector.quantize_mx(out=picked_codes[:, cols].bitcast(FP8X4), scales=picked_sc[:, cols],
                                  in_=picked_bf[c][:].rearrange("p j r -> p (j r)"))

        for r in (2, 3):
            late = sb.tile([P, T], F32, name="placed%d" % r, tag="picked_bf%d" % (r - 2), align_bytes=64)
            nc.gpsimd.memset(late[:], 0.0)
            placed.append(late)

        def product(r, c, dst):
            z = psum.tile([P, CHUNK], F32, name="z", bufs=Z_BANKS)
            for u in range(CHUNK // P):
                j0 = c * CHUNK + u * P
                nc.tensor.matmul_mx(out=z[:, u * P : (u + 1) * P], lhsT=wx_codes[:, r, :].bitcast(FP8X4),
                                    lhsT_scale=wx_sc[:, r, :], rhs=xt_codes[:, 2 * j0 : 2 * (j0 + P)].bitcast(FP4X4),
                                    rhs_scale=xt_sc[:, j0 : j0 + P], start=(u == 0), stop=False)
            slots = slice(c * CHUNK, (c + 1) * CHUNK)
            nc.tensor.matmul_mx(out=z[:], lhsT=wp_codes[:, r, :].bitcast(FP8X4), lhsT_scale=wp_sc[:, r, :],
                                rhs=picked_codes[:, slots].bitcast(FP8X4), rhs_scale=picked_sc[:, slots],
                                start=False, stop=True)
            nc.scalar.activation(dst, z[:], TANH)

        y01 = [sb.tile([P, 2, 2 * PART], F32, name="y01_%d" % u) for u in range(PARTS // 2)]
        y23 = [sb.tile([P, 2, PART], F32, name="y23_%d" % a) for a in range(PARTS)]
        y_bf = [sb.tile([P, PART, PACK], BF16, name="y_bf%d" % a, align_bytes=64) for a in range(PARTS)]
        y_codes = [sb.tile([P, PART], U32, name="y_codes%d" % a, align_bytes=64) for a in range(PARTS)]
        y_sc = sb.tile([P, T], U8, name="y_sc", align_bytes=64)

        for c in range(CHUNKS):
            for r in range(2):
                h = sb.tile([P, CHUNK], F32, name="h%d_%d" % (r, c))
                product(r, c, h[:])
                nc.vector.tensor_copy(placed[r][:].indirect(entries(write_list, c)), h[:])
        for r in (2, 3):
            h = sb.tile([P, J], F32, name="h%d" % r)
            for c in range(CHUNKS):
                product(r, c, h[:, c * CHUNK : (c + 1) * CHUNK])
            nc.vector.tensor_copy(placed[r][:].indirect(write_list[:]), h[:])

        scaled = []
        for r, tag in enumerate(("wp_raw", "wx_raw")):
            scaled_rows = sb.tile([P, T], F32, name="scaled%d" % r, tag=tag, align_bytes=64)
            nc.scalar.activation(scaled_rows[:], old_sb[r][:], COPY, scale=OLD_SCALE)
            scaled.append(scaled_rows)
        for a in range(PARTS):
            nc.scalar.activation(y23[a][:, 1, :], old_sb[2][:, a * PART : (a + 1) * PART], COPY, scale=OLD_SCALE)
        for r in range(2):
            for u in range(PARTS // 2):
                cols = slice(2 * u * PART, 2 * (u + 1) * PART)
                nc.gpsimd.tensor_tensor(y01[u][:, r, :], placed[r][:, cols], scaled[r][:, cols], ADD)
                nc.sync.dma_start(out_rows[:, r, cols], y01[u][:, r, :])
        for a in range(PARTS):
            nc.scalar.copy(y_bf[a][:, :, 0:2],
                           y01[a // 2][:, :, (a % 2) * PART : (a % 2 + 1) * PART].rearrange("p r t -> p t r"))
        for a in range(PARTS):
            cols = slice(a * PART, (a + 1) * PART)
            nc.gpsimd.tensor_tensor(y23[a][:, 0, :], placed[2][:, cols], y23[a][:, 1, :], ADD)
            nc.sync.dma_start(out_rows[:, 2, cols], y23[a][:, 0, :])
        for a in range(PARTS):
            cols = slice(a * PART, (a + 1) * PART)
            nc.vector.scalar_tensor_tensor(y23[a][:, 1, :], old_sb[3][:, cols], OLD_SCALE, placed[3][:, cols], MULT, ADD)
            nc.sync.dma_start(out_rows[:, 3, cols], y23[a][:, 1, :])
        words_out = out_1[0].rearrange("p t r -> p (t r)").bitcast(I32)

        def quantise_result(a):
            cols = slice(a * PART, (a + 1) * PART)
            nc.vector.quantize_mx(out=y_codes[a][:].bitcast(FP8X4), scales=y_sc[:, cols],
                                  in_=y_bf[a][:].rearrange("p t r -> p (t r)"))
            nc.sync.dma_start(words_out[:, cols], y_codes[a][:].bitcast(I32))

        last = PARTS - 1
        for a in range(last):
            nc.scalar.copy(y_bf[a][:, :, 2:4], y23[a][:].rearrange("p r t -> p t r"))
        quantise_result(0)
        nc.vector.tensor_copy(y_bf[last][:, :, 2:4], y23[last][:].rearrange("p r t -> p t r"))
        for a in (1, last, last - 1):
            quantise_result(a)

        for q in range(QUADS):
            eng = nc.scalar if q % 2 else nc.sync
            eng.dma_start(scale_rows(out_2, q), y_sc[QUAD * q : QUAD * q + QUAD_ROWS, :].bitcast(I32))
